import numpy as np
import ml_dtypes


def mxq(x, axis, fmt="e4m3"):
    dtype, down = {"e4m3": (ml_dtypes.float8_e4m3fn, 7), "e5m2": (ml_dtypes.float8_e5m2, 14)}[fmt]
    v = np.moveaxis(np.asarray(x, np.float32).astype(ml_dtypes.bfloat16).astype(np.float64), axis, -1)
    blocks = v.reshape(v.shape[:-1] + (-1, 32))
    amax = np.abs(blocks).max(-1, keepdims=True)
    byte = np.maximum(np.where(amax > 0, np.frexp(amax)[1] - 1 + 127, 0) - down, 1)
    scale = np.exp2(byte - 127.0)
    codes = (blocks / scale).astype(np.float32).astype(dtype).astype(np.float64)
    return np.moveaxis((codes * scale).reshape(v.shape), -1, axis)


WIDE = False


def mx_kscale(k):
    if not WIDE:
        return np.ones(k)
    levels = np.array([10, -10, 5, -5, 0])
    if k % 512:
        return np.exp2(np.random.permutation(np.resize(levels, k // 32))).repeat(32)
    a = np.empty((k // 512, 16))
    for p in range(k // 512):
        a[p, :8] = np.random.permutation(np.resize(levels, 8))
        for g in range(8):
            far = levels[np.abs(levels - a[p, g]) >= 10]
            a[p, g + 8] = far[np.random.randint(len(far))]
    return np.exp2(a.ravel()).repeat(32)


def f64(x):
    return np.asarray(x).astype(np.float64)


def striped(idx):
    return np.tile(idx.reshape(-1, 16).T, (8, 1)).astype(np.uint16)


def unstriped(offs):
    return offs[:16].T.reshape(-1).astype(np.int64)


def pack_weight(w):
    k, n = w.shape
    w = f64(np.asarray(w, np.float32).astype(ml_dtypes.bfloat16)).reshape(k // 32, 32, n)
    amax = np.abs(w).max(1)
    byte = np.clip(np.where(amax > 0, np.frexp(amax)[1] - 1 + 127 - 7, 1), 1, 254)
    scaled = (w * np.exp2(127.0 - byte)[:, None, :]).reshape(k, n).astype(np.float32)
    words = np.ascontiguousarray(scaled.reshape(k // 512, 128, 4, n).transpose(0, 1, 3, 2)).astype(ml_dtypes.float8_e4m3fn).view(np.uint8)
    return words, np.ascontiguousarray(byte.astype(np.uint8).reshape(k // 512, 16, n))


def unpack_weight(words, scales):
    g, p, n, _ = words.shape
    vals = np.ascontiguousarray(words).view(ml_dtypes.float8_e4m3fn).astype(np.float64) * np.repeat(np.exp2(scales.astype(np.float64) - 127.0), 8, axis=1)[..., None]
    return vals.transpose(0, 1, 3, 2).reshape(g * 512, n)


def relu(v):
    return np.maximum(v, 0.0)


K, T, S, V, H, N = 512, 1024, 512, 1024, 512, 128
P = 2 ** 7


def setup_inputs():
    n = np.random.standard_normal
    s = mx_kscale(K)[:, None]
    u = mx_kscale(H)
    packed = pack_weight(n((K, T)) * s)
    return {
        "x_words": packed[0],
        "x_scales": packed[1],
        "w1": (n((K, H)) / np.sqrt(K) / s * u).astype(np.float32),
        "w2": (n((H, N)) / np.sqrt(H) / u[:, None]).astype(np.float32),
        "gate": np.tile(np.random.uniform(0.5, 1.5, S), (P, 1)).astype(np.float32),
        "offs": striped(np.random.permutation(T)[:S]),
        "pos1": striped(np.random.permutation(V)[:S]),
    }


def reference(x_words, x_scales, w1, w2, gate, offs, pos1):
    h = relu(mxq(f64(w1), 0, "e4m3").T @ unpack_weight(x_words, x_scales)[:, unstriped(offs)])
    z = np.zeros((H, V))
    z[:, unstriped(pos1)] = f64(gate)[:1] * h
    return mxq(f64(w2), 0, "e4m3").T @ mxq(z, 0, "e4m3")

@@ -1,0 +1,160 @@
+from contextlib import ExitStack
+
+import concourse.mybir as mybir
+
+K, T, S, V, H, N = 512, 1024, 512, 1024, 512, 128
+FLOPS = 2 * K * H * S + 2 * H * N * V
+
+F32 = mybir.dt.float32
+BF16 = mybir.dt.bfloat16
+I32 = mybir.dt.int32
+U32 = mybir.dt.uint32
+U16 = mybir.dt.uint16
+U8 = mybir.dt.uint8
+FP8X4 = mybir.dt.float8_e4m3fn_x4
+RELU = mybir.ActivationFunctionType.Relu
+MULT = mybir.AluOpType.mult
+
+P = 128
+PACK = 4
+CHUNK = 256
+
+
+def tile_picked_voxel_relu_p_kernel(tc, x_words, x_scales, w1, w2, gate, offs, pos1, out):
+    nc = tc.nc
+    with ExitStack() as ctx:
+        keep = ctx.enter_context(tc.tile_pool(name="keep", bufs=1))
+        psum = ctx.enter_context(tc.psum_pool(name="psum", bufs=8))
+
+        point_list = keep.tile([P, S // 16], U16)
+        cell_list = keep.tile([P, S // 16], U16)
+        word_table = keep.tile([P, T], I32, align_bytes=64)
+        scale_table = keep.tile([P, T // 4], I32, align_bytes=64)
+        w1_raw = [keep.tile([P, PACK, H // 2], F32, name="w1_raw%d" % u) for u in range(2)]
+        w2_raw = keep.tile([P, PACK, N], F32)
+        gates = keep.tile([P, S], F32)
+
+        nc.gpsimd.memset(scale_table[:], 0)
+        nc.sync.dma_start(point_list[:], offs)
+        nc.sync.dma_start(word_table[:], x_words[0].rearrange("p c r -> p (c r)").bitcast(I32))
+        for q in range(4):
+            nc.sync.dma_start(scale_table[32 * q : 32 * q + 4, :], x_scales[0, 4 * q : 4 * q + 4, :].bitcast(I32))
+        w1_rows = w1.rearrange("(p j) c -> p j c", j=PACK)
+        for u in range(2):
+            nc.sync.dma_start(w1_raw[u][:], w1_rows[:, :, u * (H // 2) : (u + 1) * (H // 2)])
+        nc.sync.dma_start(cell_list[:], pos1)
+        nc.sync.dma_start(gates[:], gate)
+        nc.sync.dma_start(w2_raw[:], w2.rearrange("(p j) n -> p j n", j=PACK))
+
+        narrow = {t: keep.tile([P, V], F32, name="narrow%d" % t) for t in (1, 3)}
+        wide = {t: keep.tile([P, 2 * V], F32, name="wide%d" % t) for t in (0, 2)}
+        nc.vector.memset(narrow[1][:], 0.0)
+        nc.scalar.activation(narrow[3][:], narrow[1][:], RELU)
+        nc.gpsimd.memset(wide[0][:, :V], 0.0)
+        nc.gpsimd.memset(wide[2][:, :V], 0.0)
+
+        x_codes = keep.tile([P, S], U32, align_bytes=64)
+        x_plane = keep.tile([P, S], U8, align_bytes=64)
+        nc.vector.tensor_copy(x_codes[:], word_table[:].bitcast(U32).indirect(point_list[:]))
+        nc.vector.tensor_copy(x_plane[:], scale_table[:].bitcast(U8).indirect(point_list[:]))
+
+        w1_grouped = keep.tile([P, PACK, P, PACK], BF16, align_bytes=64)
+        for u, copy in enumerate((nc.scalar.copy, nc.vector.tensor_copy)):
+            copy(
+                w1_grouped[:, :, 64 * u : 64 * u + 64, :].rearrange("p t m j -> p m t j"),
+                w1_raw[u][:].rearrange("p j (m t) -> p m t j", t=PACK),
+            )
+        w1_codes = keep.tile([P, H], U32, align_bytes=64)
+        w1_plane = keep.tile([P, H], U8, align_bytes=64)
+
+        def quantize_w1(t0, t1):
+            nc.vector.quantize_mx(
+                out=w1_codes[:, P * t0 : P * t1].bitcast(FP8X4),
+                scales=w1_plane[:, P * t0 : P * t1],
+                in_=w1_grouped[:, t0:t1, :, :].rearrange("p t m j -> p (t m j)"),
+            )
+
+        hidden = {t: keep.tile([P, S], F32, name="hidden%d" % t) for t in range(PACK)}
+
+        def first_layer(t, lo, hi):
+            acc = psum.tile([P, hi - lo], F32, name="acc")
+            nc.tensor.matmul_mx(
+                out=acc[:],
+                lhsT=w1_codes[:, P * t : P * (t + 1)].bitcast(FP8X4),
+                lhsT_scale=w1_plane[:, P * t : P * (t + 1)],
+                rhs=x_codes[:, lo:hi].bitcast(FP8X4),
+                rhs_scale=x_plane[:, lo:hi],
+                start=True,
+                stop=True,
+            )
+            nc.scalar.activation(hidden[t][:, lo:hi], acc[:], RELU)
+
+        def scatter(window, t, lo, hi):
+            nc.vector.tensor_tensor(
+                window[:].indirect(cell_list[:, lo // 16 : hi // 16]), hidden[t][:, lo:hi], gates[:, lo:hi], MULT
+            )
+
+        quantize_w1(1, 2)
+        first_layer(1, 0, S // 2)
+        first_layer(1, S // 2, S)
+        quantize_w1(2, 4)
+        quantize_w1(0, 1)
+        for t in (3, 0, 2):
+            first_layer(t, 0, S)
+
+        w2_grouped = keep.tile([P, N, PACK], BF16, align_bytes=64)
+        nc.scalar.copy(w2_grouped[:], w2_raw[:].rearrange("p j n -> p n j"))
+
+        scatter(narrow[1], 1, 0, S // 2)
+        scatter(narrow[1], 1, S // 2, S)
+        nc.scalar.copy(wide[0][:, V:], narrow[1][:])
+        w2_codes = keep.tile([P, N], U32, align_bytes=64)
+        w2_plane = keep.tile([P, N], U8, align_bytes=64)
+        nc.vector.quantize_mx(
+            out=w2_codes[:].bitcast(FP8X4), scales=w2_plane[:], in_=w2_grouped[:].rearrange("p n j -> p (n j)")
+        )
+        scatter(narrow[3], 3, 0, S)
+        nc.scalar.copy(wide[2][:, V:], narrow[3][:])
+        scatter(wide[0], 0, 0, S)
+
+        z_grouped = keep.tile([P, V, PACK], BF16, align_bytes=64)
+
+        def interleave(copy, t, lo, hi):
+            copy(z_grouped[:, lo:hi, t : t + 2], wide[t][:].rearrange("p (e v) -> p v e", e=2)[:, lo:hi, :])
+
+        interleave(nc.scalar.copy, 0, 0, V // 2)
+        interleave(nc.scalar.copy, 0, V // 2, V)
+        scatter(wide[2], 2, 0, S)
+
+        z_codes = keep.tile([P, V], U32, align_bytes=64)
+        z_plane = keep.tile([P, V], U8, align_bytes=64)
+        result = keep.tile([P, V], F32)
+
+        def second_layer(c, copy):
+            cells = slice(c * CHUNK, (c + 1) * CHUNK)
+            nc.vector.quantize_mx(
+                out=z_codes[:, cells].bitcast(FP8X4),
+                scales=z_plane[:, cells],
+                in_=z_grouped[:, cells, :].rearrange("p v t -> p (v t)"),
+            )
+            acc = psum.tile([P, CHUNK], F32, name="acc")
+            nc.tensor.matmul_mx(
+                out=acc[:],
+                lhsT=w2_codes[:].bitcast(FP8X4),
+                lhsT_scale=w2_plane[:],
+                rhs=z_codes[:, cells].bitcast(FP8X4),
+                rhs_scale=z_plane[:, cells],
+                start=True,
+                stop=True,
+            )
+            copy(result[:, cells], acc[:])
+            nc.sync.dma_start(out[:, cells], result[:, cells])
+
+        interleave(nc.vector.tensor_copy, 2, 0, CHUNK)
+        interleave(nc.scalar.copy, 2, 2 * CHUNK, 3 * CHUNK)
+        interleave(nc.vector.tensor_copy, 2, CHUNK, 2 * CHUNK)
+        interleave(nc.scalar.copy, 2, 3 * CHUNK, 4 * CHUNK)
+        second_layer(0, nc.scalar.copy)
+        second_layer(1, nc.scalar.copy)
+        second_layer(2, nc.scalar.copy)
+        second_layer(3, nc.vector.tensor_copy)

@@ -17,7 +17,6 @@ MULT = mybir.AluOpType.mult
 
 P = 128
 PACK = 4
-CHUNK = 256
 
 
 def tile_picked_voxel_relu_p_kernel(tc, x_words, x_scales, w1, w2, gate, offs, pos1, out):
@@ -26,135 +25,147 @@ def tile_picked_voxel_relu_p_kernel(tc, x_words, x_scales, w1, w2, gate, offs, p
         keep = ctx.enter_context(tc.tile_pool(name="keep", bufs=1))
         psum = ctx.enter_context(tc.psum_pool(name="psum", bufs=8))
 
-        point_list = keep.tile([P, S // 16], U16)
-        cell_list = keep.tile([P, S // 16], U16)
-        word_table = keep.tile([P, T], I32, align_bytes=64)
-        scale_table = keep.tile([P, T // 4], I32, align_bytes=64)
-        w1_raw = [keep.tile([P, PACK, H // 2], F32, name="w1_raw%d" % u) for u in range(2)]
-        w2_raw = keep.tile([P, PACK, N], F32)
-        gates = keep.tile([P, S], F32)
-
-        nc.gpsimd.memset(scale_table[:], 0)
-        nc.sync.dma_start(point_list[:], offs)
-        nc.sync.dma_start(word_table[:], x_words[0].rearrange("p c r -> p (c r)").bitcast(I32))
-        for q in range(4):
-            nc.sync.dma_start(scale_table[32 * q : 32 * q + 4, :], x_scales[0, 4 * q : 4 * q + 4, :].bitcast(I32))
-        w1_rows = w1.rearrange("(p j) c -> p j c", j=PACK)
-        for u in range(2):
-            nc.sync.dma_start(w1_raw[u][:], w1_rows[:, :, u * (H // 2) : (u + 1) * (H // 2)])
-        nc.sync.dma_start(cell_list[:], pos1)
-        nc.sync.dma_start(gates[:], gate)
-        nc.sync.dma_start(w2_raw[:], w2.rearrange("(p j) n -> p j n", j=PACK))
-
-        narrow = {t: keep.tile([P, V], F32, name="narrow%d" % t) for t in (1, 3)}
-        wide = {t: keep.tile([P, 2 * V], F32, name="wide%d" % t) for t in (0, 2)}
-        nc.vector.memset(narrow[1][:], 0.0)
-        nc.scalar.activation(narrow[3][:], narrow[1][:], RELU)
-        nc.gpsimd.memset(wide[0][:, :V], 0.0)
-        nc.gpsimd.memset(wide[2][:, :V], 0.0)
-
-        x_codes = keep.tile([P, S], U32, align_bytes=64)
-        x_plane = keep.tile([P, S], U8, align_bytes=64)
-        nc.vector.tensor_copy(x_codes[:], word_table[:].bitcast(U32).indirect(point_list[:]))
-        nc.vector.tensor_copy(x_plane[:], scale_table[:].bitcast(U8).indirect(point_list[:]))
-
-        w1_grouped = keep.tile([P, PACK, P, PACK], BF16, align_bytes=64)
-        for u, copy in enumerate((nc.scalar.copy, nc.vector.tensor_copy)):
-            copy(
-                w1_grouped[:, :, 64 * u : 64 * u + 64, :].rearrange("p t m j -> p m t j"),
-                w1_raw[u][:].rearrange("p j (m t) -> p m t j", t=PACK),
-            )
-        w1_codes = keep.tile([P, H], U32, align_bytes=64)
-        w1_plane = keep.tile([P, H], U8, align_bytes=64)
-
-        def quantize_w1(t0, t1):
+        def quantize(codes, plane, grouped, lo, hi):
             nc.vector.quantize_mx(
-                out=w1_codes[:, P * t0 : P * t1].bitcast(FP8X4),
-                scales=w1_plane[:, P * t0 : P * t1],
-                in_=w1_grouped[:, t0:t1, :, :].rearrange("p t m j -> p (t m j)"),
+                out=codes[:, lo:hi].bitcast(FP8X4),
+                scales=plane[:, lo:hi],
+                in_=grouped[:, lo:hi, :].rearrange("p c j -> p (c j)"),
             )
 
-        hidden = {t: keep.tile([P, S], F32, name="hidden%d" % t) for t in range(PACK)}
-
-        def first_layer(t, lo, hi):
-            acc = psum.tile([P, hi - lo], F32, name="acc")
+        def product(acc, w_codes, w_plane, w_cols, codes, plane, lo, hi):
             nc.tensor.matmul_mx(
-                out=acc[:],
-                lhsT=w1_codes[:, P * t : P * (t + 1)].bitcast(FP8X4),
-                lhsT_scale=w1_plane[:, P * t : P * (t + 1)],
-                rhs=x_codes[:, lo:hi].bitcast(FP8X4),
-                rhs_scale=x_plane[:, lo:hi],
+                out=acc,
+                lhsT=w_codes[:, w_cols].bitcast(FP8X4),
+                lhsT_scale=w_plane[:, w_cols],
+                rhs=codes[:, lo:hi].bitcast(FP8X4),
+                rhs_scale=plane[:, lo:hi],
                 start=True,
                 stop=True,
             )
-            nc.scalar.activation(hidden[t][:, lo:hi], acc[:], RELU)
 
-        def scatter(window, t, lo, hi):
-            nc.vector.tensor_tensor(
-                window[:].indirect(cell_list[:, lo // 16 : hi // 16]), hidden[t][:, lo:hi], gates[:, lo:hi], MULT
+        point_list = keep.tile([P, S // 16], U16)
+        cell_list = keep.tile([P, S // 16], U16)
+        word_table = keep.tile([P, T], I32, align_bytes=64, tag="late")
+        scale_rows = keep.tile([P, T // 4], I32, align_bytes=64)
+        scale_table = keep.tile([P, T // 4], I32, align_bytes=64)
+        w1_raw = keep.tile([P, PACK, H], F32, tag="raw")
+        gates = keep.tile([P, S], F32)
+
+        nc.sync.dma_start(point_list[:], offs)
+        for q, queue in enumerate((nc.sync, nc.scalar, nc.sync, nc.scalar)):
+            queue.dma_start(scale_rows[32 * q : 32 * q + 4, :], x_scales[0, 4 * q : 4 * q + 4, :].bitcast(I32))
+        nc.sync.dma_start(w1_raw[:], w1.rearrange("(p j) c -> p j c", j=PACK))
+        nc.sync.dma_start(word_table[:], x_words[0].rearrange("p c r -> p (c r)").bitcast(I32))
+        nc.sync.dma_start(cell_list[:], pos1)
+        nc.sync.dma_start(gates[:], gate)
+
+        narrow = {o: keep.tile([P, V], F32, name="narrow%d" % o) for o in (2, 3)}
+        wide = {0: keep.tile([P, 2 * V], F32, name="wide0")}
+        zero = keep.tile([P, 8], F32)
+        nc.gpsimd.memset(scale_table[:], 0)
+        nc.gpsimd.memset(wide[0][:, :V], 0.0)
+        nc.vector.memset(zero[:], 0.0)
+        nc.vector.memset(narrow[2][:], 0.0)
+        nc.scalar.activation(narrow[3][:], zero[:, 0:1].to_broadcast([P, V]), RELU)
+
+        for q in range(4):
+            nc.vector.tensor_copy(scale_table[32 * q : 32 * q + 4, :], scale_rows[32 * q : 32 * q + 4, :])
+        x_codes = keep.tile([P, S], U32, align_bytes=64, tag="last")
+        x_plane = keep.tile([P, S], U8, align_bytes=64)
+        nc.vector.tensor_copy(x_plane[:], scale_table[:].bitcast(U8).indirect(point_list[:]))
+
+        w1_grouped = keep.tile([P, H, PACK], BF16, align_bytes=64)
+
+        def group_w1(copy, o, lo, hi):
+            copy(
+                w1_grouped[:].rearrange("p (o m) j -> p m j o", o=PACK)[:, lo:hi, :, o : o + 2],
+                w1_raw[:].rearrange("p j (m o) -> p m j o", o=PACK)[:, lo:hi, :, o : o + 2],
             )
 
-        quantize_w1(1, 2)
-        first_layer(1, 0, S // 2)
-        first_layer(1, S // 2, S)
-        quantize_w1(2, 4)
-        quantize_w1(0, 1)
-        for t in (3, 0, 2):
-            first_layer(t, 0, S)
+        w1_codes, w1_plane = {}, {}
+
+        def quantize_w1(o, tag):
+            w1_codes[o] = keep.tile([P, 2 * P], U32, align_bytes=64, name="w1_codes%d" % o, tag=tag)
+            w1_plane[o] = keep.tile([P, 2 * P], U8, align_bytes=64, name="w1_plane%d" % o)
+            quantize(w1_codes[o], w1_plane[o], w1_grouped[:, P * o : P * (o + 2), :], 0, 2 * P)
+
+        group_w1(nc.vector.tensor_copy, 2, 0, 84)
+        group_w1(nc.scalar.copy, 2, 84, P)
+        group_w1(nc.vector.tensor_copy, 0, 0, 48)
+        group_w1(nc.scalar.copy, 0, 48, P)
+        quantize_w1(2, "early")
+
+        w2_raw = keep.tile([P, PACK, N], F32, tag="raw")
+        nc.sync.dma_start(w2_raw[:], w2.rearrange("(p j) n -> p j n", j=PACK))
+
+        def gather_words(lo, hi):
+            nc.vector.tensor_copy(x_codes[:, lo:hi], word_table[:].bitcast(U32).indirect(point_list[:, lo // 16 : hi // 16]))
+
+        hidden = {o: keep.tile([P, S], F32, name="hidden%d" % o) for o in range(PACK)}
+
+        def first_layer(o, *edges):
+            acc = psum.tile([P, edges[-1] - edges[0]], F32, name="acc")
+            for lo, hi in zip(edges, edges[1:]):
+                product(acc[:, lo - edges[0] : hi - edges[0]], w1_codes[o - o % 2], w1_plane[o - o % 2], slice(P * (o % 2), P * (o % 2 + 1)), x_codes, x_plane, lo, hi)
+            nc.scalar.activation(hidden[o][:, edges[0] : edges[-1]], acc[:], RELU)
+
+        def scatter(window, o, lo, hi):
+            nc.vector.tensor_tensor(
+                window[:].indirect(cell_list[:, lo // 16 : hi // 16]), hidden[o][:, lo:hi], gates[:, lo:hi], MULT
+            )
+
+        gather_words(0, 128)
+        gather_words(128, S)
+        for o in (2, 3):
+            first_layer(o, 0, 128)
+        quantize_w1(0, "late")
+        for o in (2, 3):
+            first_layer(o, 128, 384, S)
+        for o in (0, 1):
+            first_layer(o, 0, S)
+        wide[1] = keep.tile([P, 2 * V], F32, name="wide1", align_bytes=64, tag="last")
+        nc.scalar.copy(wide[1][:, :V], zero[:, 0:1].to_broadcast([P, V]))
+        scatter(narrow[2], 2, 0, 128)
+        scatter(narrow[3], 3, 0, 128)
+        scatter(narrow[2], 2, 128, S)
+        scatter(narrow[3], 3, 128, S)
+        nc.scalar.copy(wide[0][:, V:], narrow[2][:])
+        nc.scalar.copy(wide[1][:, V:], narrow[3][:])
+        scatter(wide[0], 0, 0, S)
 
         w2_grouped = keep.tile([P, N, PACK], BF16, align_bytes=64)
-        nc.scalar.copy(w2_grouped[:], w2_raw[:].rearrange("p j n -> p n j"))
-
-        scatter(narrow[1], 1, 0, S // 2)
-        scatter(narrow[1], 1, S // 2, S)
-        nc.scalar.copy(wide[0][:, V:], narrow[1][:])
+        nc.scalar.copy(
+            w2_grouped[:].rearrange("p n (a e) -> p n a e", e=2), w2_raw[:].rearrange("p (e a) n -> p n a e", e=2)
+        )
         w2_codes = keep.tile([P, N], U32, align_bytes=64)
         w2_plane = keep.tile([P, N], U8, align_bytes=64)
-        nc.vector.quantize_mx(
-            out=w2_codes[:].bitcast(FP8X4), scales=w2_plane[:], in_=w2_grouped[:].rearrange("p n j -> p (n j)")
-        )
-        scatter(narrow[3], 3, 0, S)
-        nc.scalar.copy(wide[2][:, V:], narrow[3][:])
-        scatter(wide[0], 0, 0, S)
+        quantize(w2_codes, w2_plane, w2_grouped, 0, N)
 
         z_grouped = keep.tile([P, V, PACK], BF16, align_bytes=64)
 
-        def interleave(copy, t, lo, hi):
-            copy(z_grouped[:, lo:hi, t : t + 2], wide[t][:].rearrange("p (e v) -> p v e", e=2)[:, lo:hi, :])
+        def interleave(copy, a, lo, hi):
+            copy(z_grouped[:, lo:hi, 2 * a : 2 * a + 2], wide[a][:].rearrange("p (e v) -> p v e", e=2)[:, lo:hi, :])
 
         interleave(nc.scalar.copy, 0, 0, V // 2)
         interleave(nc.scalar.copy, 0, V // 2, V)
-        scatter(wide[2], 2, 0, S)
-
+        scatter(wide[1], 1, 0, S)
         z_codes = keep.tile([P, V], U32, align_bytes=64)
         z_plane = keep.tile([P, V], U8, align_bytes=64)
         result = keep.tile([P, V], F32)
 
-        def second_layer(c, copy):
-            cells = slice(c * CHUNK, (c + 1) * CHUNK)
-            nc.vector.quantize_mx(
-                out=z_codes[:, cells].bitcast(FP8X4),
-                scales=z_plane[:, cells],
-                in_=z_grouped[:, cells, :].rearrange("p v t -> p (v t)"),
-            )
-            acc = psum.tile([P, CHUNK], F32, name="acc")
-            nc.tensor.matmul_mx(
-                out=acc[:],
-                lhsT=w2_codes[:].bitcast(FP8X4),
-                lhsT_scale=w2_plane[:],
-                rhs=z_codes[:, cells].bitcast(FP8X4),
-                rhs_scale=z_plane[:, cells],
-                start=True,
-                stop=True,
-            )
-            copy(result[:, cells], acc[:])
-            nc.sync.dma_start(out[:, cells], result[:, cells])
+        def quantize_z(lo, hi):
+            quantize(z_codes, z_plane, z_grouped, lo, hi)
 
-        interleave(nc.vector.tensor_copy, 2, 0, CHUNK)
-        interleave(nc.scalar.copy, 2, 2 * CHUNK, 3 * CHUNK)
-        interleave(nc.vector.tensor_copy, 2, CHUNK, 2 * CHUNK)
-        interleave(nc.scalar.copy, 2, 3 * CHUNK, 4 * CHUNK)
-        second_layer(0, nc.scalar.copy)
-        second_layer(1, nc.scalar.copy)
-        second_layer(2, nc.scalar.copy)
-        second_layer(3, nc.vector.tensor_copy)
+        def second_layer(copy, lo, hi):
+            acc = psum.tile([P, hi - lo], F32, name="acc")
+            product(acc[:], w2_codes, w2_plane, slice(0, N), z_codes, z_plane, lo, hi)
+            copy(result[:, lo:hi], acc[:])
+            nc.sync.dma_start(out[:, lo:hi], result[:, lo:hi])
+
+        interleave(nc.vector.tensor_copy, 1, 0, 256)
+        interleave(nc.scalar.copy, 1, 512, 768)
+        interleave(nc.vector.tensor_copy, 1, 256, 512)
+        interleave(nc.scalar.copy, 1, 768, 1024)
+        for c, copy in enumerate((nc.scalar.copy, nc.scalar.copy, nc.scalar.copy, nc.vector.tensor_copy)):
+            quantize_z(256 * c, 256 * (c + 1))
+            second_layer(copy, 256 * c, 256 * (c + 1))

@@ -62,10 +62,10 @@ def tile_picked_voxel_relu_p_kernel(tc, x_words, x_scales, w1, w2, gate, offs, p
         narrow = {o: keep.tile([P, V], F32, name="narrow%d" % o) for o in (2, 3)}
         wide = {0: keep.tile([P, 2 * V], F32, name="wide0")}
         zero = keep.tile([P, 8], F32)
-        nc.gpsimd.memset(scale_table[:], 0)
-        nc.gpsimd.memset(wide[0][:, :V], 0.0)
         nc.vector.memset(zero[:], 0.0)
+        nc.vector.memset(scale_table[:], 0)
         nc.vector.memset(narrow[2][:], 0.0)
+        nc.vector.memset(wide[0][:, :V], 0.0)
         nc.scalar.activation(narrow[3][:], zero[:, 0:1].to_broadcast([P, V]), RELU)
 
         for q in range(4):

@@ -156,16 +156,28 @@ def tile_picked_voxel_relu_p_kernel(tc, x_words, x_scales, w1, w2, gate, offs, p
         def quantize_z(lo, hi):
             quantize(z_codes, z_plane, z_grouped, lo, hi)
 
-        def second_layer(copy, lo, hi):
-            acc = psum.tile([P, hi - lo], F32, name="acc")
-            product(acc[:], w2_codes, w2_plane, slice(0, N), z_codes, z_plane, lo, hi)
-            copy(result[:, lo:hi], acc[:])
+        def second_layer(copy, *edges):
+            acc = psum.tile([P, edges[-1] - edges[0]], F32, name="acc")
+            for lo, hi in zip(edges, edges[1:]):
+                product(acc[:, lo - edges[0] : hi - edges[0]], w2_codes, w2_plane, slice(0, N), z_codes, z_plane, lo, hi)
+            copy(result[:, edges[0] : edges[-1]], acc[:])
+
+        def store(lo, hi):
             nc.sync.dma_start(out[:, lo:hi], result[:, lo:hi])
 
         interleave(nc.vector.tensor_copy, 1, 0, 256)
-        interleave(nc.scalar.copy, 1, 512, 768)
-        interleave(nc.vector.tensor_copy, 1, 256, 512)
+        interleave(nc.scalar.copy, 1, 576, 768)
+        interleave(nc.vector.tensor_copy, 1, 256, 576)
         interleave(nc.scalar.copy, 1, 768, 1024)
-        for c, copy in enumerate((nc.scalar.copy, nc.scalar.copy, nc.scalar.copy, nc.vector.tensor_copy)):
-            quantize_z(256 * c, 256 * (c + 1))
-            second_layer(copy, 256 * c, 256 * (c + 1))
+        quantize_z(0, 256)
+        second_layer(nc.scalar.copy, 0, 256)
+        store(0, 256)
+        quantize_z(256, 512)
+        second_layer(nc.scalar.copy, 256, 512)
+        store(256, 512)
+        quantize_z(512, 768)
+        second_layer(nc.scalar.copy, 512, 768)
+        store(512, 768)
+        quantize_z(768, 1024)
+        second_layer(nc.vector.tensor_copy, 768, 1024)
+        store(768, 1024)

@@ -45,7 +45,7 @@ def tile_picked_voxel_relu_p_kernel(tc, x_words, x_scales, w1, w2, gate, offs, p
 
         point_list = keep.tile([P, S // 16], U16)
         cell_list = keep.tile([P, S // 16], U16)
-        word_table = keep.tile([P, T], I32, align_bytes=64, tag="late")
+        word_table = keep.tile([P, T], I32, align_bytes=64)
         scale_rows = keep.tile([P, T // 4], I32, align_bytes=64)
         scale_table = keep.tile([P, T // 4], I32, align_bytes=64)
         w1_raw = keep.tile([P, PACK, H], F32, tag="raw")
@@ -91,8 +91,7 @@ def tile_picked_voxel_relu_p_kernel(tc, x_words, x_scales, w1, w2, gate, offs, p
 
         group_w1(nc.vector.tensor_copy, 2, 0, 84)
         group_w1(nc.scalar.copy, 2, 84, P)
-        group_w1(nc.vector.tensor_copy, 0, 0, 48)
-        group_w1(nc.scalar.copy, 0, 48, P)
+        group_w1(nc.scalar.copy, 0, 0, P)
         quantize_w1(2, "early")
 
         w2_raw = keep.tile([P, PACK, N], F32, tag="raw")
@@ -118,7 +117,7 @@ def tile_picked_voxel_relu_p_kernel(tc, x_words, x_scales, w1, w2, gate, offs, p
         gather_words(128, S)
         for o in (2, 3):
             first_layer(o, 0, 128)
-        quantize_w1(0, "late")
+        quantize_w1(0, "second")
         for o in (2, 3):
             first_layer(o, 128, 384, S)
         for o in (0, 1):

@@ -100,7 +100,7 @@ def tile_picked_voxel_relu_p_kernel(tc, x_words, x_scales, w1, w2, gate, offs, p
         def gather_words(lo, hi):
             nc.vector.tensor_copy(x_codes[:, lo:hi], word_table[:].bitcast(U32).indirect(point_list[:, lo // 16 : hi // 16]))
 
-        hidden = {o: keep.tile([P, S], F32, name="hidden%d" % o) for o in range(PACK)}
+        hidden = {o: keep.tile([P, S], F32, name="hidden%d" % o, align_bytes=64) for o in range(PACK)}
 
         def first_layer(o, *edges):
             acc = psum.tile([P, edges[-1] - edges[0]], F32, name="acc")
@@ -136,9 +136,6 @@ def tile_picked_voxel_relu_p_kernel(tc, x_words, x_scales, w1, w2, gate, offs, p
         nc.scalar.copy(
             w2_grouped[:].rearrange("p n (a e) -> p n a e", e=2), w2_raw[:].rearrange("p (e a) n -> p n a e", e=2)
         )
-        w2_codes = keep.tile([P, N], U32, align_bytes=64)
-        w2_plane = keep.tile([P, N], U8, align_bytes=64)
-        quantize(w2_codes, w2_plane, w2_grouped, 0, N)
 
         z_grouped = keep.tile([P, V, PACK], BF16, align_bytes=64)
 
@@ -148,6 +145,9 @@ def tile_picked_voxel_relu_p_kernel(tc, x_words, x_scales, w1, w2, gate, offs, p
         interleave(nc.scalar.copy, 0, 0, V // 2)
         interleave(nc.scalar.copy, 0, V // 2, V)
         scatter(wide[1], 1, 0, S)
+        w2_codes = keep.tile([P, N], U32, align_bytes=64, tag="hidden0")
+        w2_plane = keep.tile([P, N], U8, align_bytes=64)
+        quantize(w2_codes, w2_plane, w2_grouped, 0, N)
         z_codes = keep.tile([P, V], U32, align_bytes=64)
         z_plane = keep.tile([P, V], U8, align_bytes=64)
         result = keep.tile([P, V], F32)
@@ -165,8 +165,8 @@ def tile_picked_voxel_relu_p_kernel(tc, x_words, x_scales, w1, w2, gate, offs, p
             nc.sync.dma_start(out[:, lo:hi], result[:, lo:hi])
 
         interleave(nc.vector.tensor_copy, 1, 0, 256)
-        interleave(nc.scalar.copy, 1, 576, 768)
-        interleave(nc.vector.tensor_copy, 1, 256, 576)
+        interleave(nc.scalar.copy, 1, 528, 768)
+        interleave(nc.vector.tensor_copy, 1, 256, 528)
         interleave(nc.scalar.copy, 1, 768, 1024)
         quantize_z(0, 256)
         second_layer(nc.scalar.copy, 0, 256)

@@ -177,6 +177,8 @@ def tile_picked_voxel_relu_p_kernel(tc, x_words, x_scales, w1, w2, gate, offs, p
         quantize_z(512, 768)
         second_layer(nc.scalar.copy, 512, 768)
         store(512, 768)
-        quantize_z(768, 1024)
-        second_layer(nc.vector.tensor_copy, 768, 1024)
+        quantize_z(768, 896)
+        second_layer(nc.vector.tensor_copy, 768, 896)
+        quantize_z(896, 1024)
+        second_layer(nc.vector.tensor_copy, 896, 1024)
         store(768, 1024)

@@ -165,9 +165,11 @@ def tile_picked_voxel_relu_p_kernel(tc, x_words, x_scales, w1, w2, gate, offs, p
             nc.sync.dma_start(out[:, lo:hi], result[:, lo:hi])
 
         interleave(nc.vector.tensor_copy, 1, 0, 256)
-        interleave(nc.scalar.copy, 1, 528, 768)
-        interleave(nc.vector.tensor_copy, 1, 256, 528)
-        interleave(nc.scalar.copy, 1, 768, 1024)
+        interleave(nc.scalar.copy, 1, 480, 512)
+        interleave(nc.vector.tensor_copy, 1, 256, 480)
+        interleave(nc.scalar.copy, 1, 512, 768)
+        interleave(nc.scalar.copy, 1, 768, 896)
+        interleave(nc.scalar.copy, 1, 896, 1024)
         quantize_z(0, 256)
         second_layer(nc.scalar.copy, 0, 256)
         store(0, 256)

@@ -12,7 +12,8 @@ U32 = mybir.dt.uint32
 U16 = mybir.dt.uint16
 U8 = mybir.dt.uint8
 FP8X4 = mybir.dt.float8_e4m3fn_x4
-RELU = mybir.ActivationFunctionType.Relu
+COPY = mybir.ActivationFunctionType.Copy
+MAX = mybir.AluOpType.max
 MULT = mybir.AluOpType.mult
 
 P = 128
@@ -48,7 +49,7 @@ def tile_picked_voxel_relu_p_kernel(tc, x_words, x_scales, w1, w2, gate, offs, p
         word_table = keep.tile([P, T], I32, align_bytes=64)
         scale_rows = keep.tile([P, T // 4], I32, align_bytes=64)
         scale_table = keep.tile([P, T // 4], I32, align_bytes=64)
-        w1_raw = keep.tile([P, PACK, H], F32, tag="raw")
+        w1_raw = keep.tile([P, PACK, H], F32)
         gates = keep.tile([P, S], F32)
 
         nc.sync.dma_start(point_list[:], offs)
@@ -57,20 +58,22 @@ def tile_picked_voxel_relu_p_kernel(tc, x_words, x_scales, w1, w2, gate, offs, p
         nc.sync.dma_start(w1_raw[:], w1.rearrange("(p j) c -> p j c", j=PACK))
         nc.sync.dma_start(word_table[:], x_words[0].rearrange("p c r -> p (c r)").bitcast(I32))
         nc.sync.dma_start(cell_list[:], pos1)
-        nc.sync.dma_start(gates[:], gate)
+        nc.sync.dma_start(gates[:, :256], gate[:, :256])
+        nc.sync.dma_start(gates[:, 256:], gate[:, 256:])
 
         narrow = {o: keep.tile([P, V], F32, name="narrow%d" % o) for o in (2, 3)}
-        wide = {0: keep.tile([P, 2 * V], F32, name="wide0")}
+        wide = {a: keep.tile([P, 2 * V], F32, name="wide%d" % a) for a in (0, 1)}
         zero = keep.tile([P, 8], F32)
         nc.vector.memset(zero[:], 0.0)
         nc.vector.memset(scale_table[:], 0)
         nc.vector.memset(narrow[2][:], 0.0)
         nc.vector.memset(wide[0][:, :V], 0.0)
-        nc.scalar.activation(narrow[3][:], zero[:, 0:1].to_broadcast([P, V]), RELU)
+        nc.scalar.activation(narrow[3][:], zero[:, 0:1].to_broadcast([P, V]), COPY)
+        nc.scalar.activation(wide[1][:, :V], zero[:, 0:1].to_broadcast([P, V]), COPY)
 
         for q in range(4):
             nc.vector.tensor_copy(scale_table[32 * q : 32 * q + 4, :], scale_rows[32 * q : 32 * q + 4, :])
-        x_codes = keep.tile([P, S], U32, align_bytes=64, tag="last")
+        x_codes = keep.tile([P, S], U32, align_bytes=64)
         x_plane = keep.tile([P, S], U8, align_bytes=64)
         nc.vector.tensor_copy(x_plane[:], scale_table[:].bitcast(U8).indirect(point_list[:]))
 
@@ -94,46 +97,45 @@ def tile_picked_voxel_relu_p_kernel(tc, x_words, x_scales, w1, w2, gate, offs, p
         group_w1(nc.scalar.copy, 0, 0, P)
         quantize_w1(2, "early")
 
-        w2_raw = keep.tile([P, PACK, N], F32, tag="raw")
+        w2_raw = keep.tile([P, PACK, N], F32)
         nc.sync.dma_start(w2_raw[:], w2.rearrange("(p j) n -> p j n", j=PACK))
 
         def gather_words(lo, hi):
             nc.vector.tensor_copy(x_codes[:, lo:hi], word_table[:].bitcast(U32).indirect(point_list[:, lo // 16 : hi // 16]))
 
-        hidden = {o: keep.tile([P, S], F32, name="hidden%d" % o, align_bytes=64) for o in range(PACK)}
+        hidden = {}
 
-        def first_layer(o, *edges):
+        def first_layer(o, *edges, tag=""):
+            hidden[o, edges[0]] = keep.tile([P, edges[-1] - edges[0]], F32, name="hidden%d_%d" % (o, edges[0]), tag=tag)
             acc = psum.tile([P, edges[-1] - edges[0]], F32, name="acc")
             for lo, hi in zip(edges, edges[1:]):
                 product(acc[:, lo - edges[0] : hi - edges[0]], w1_codes[o - o % 2], w1_plane[o - o % 2], slice(P * (o % 2), P * (o % 2 + 1)), x_codes, x_plane, lo, hi)
-            nc.scalar.activation(hidden[o][:, edges[0] : edges[-1]], acc[:], RELU)
-
-        def scatter(window, o, lo, hi):
-            nc.vector.tensor_tensor(
-                window[:].indirect(cell_list[:, lo // 16 : hi // 16]), hidden[o][:, lo:hi], gates[:, lo:hi], MULT
+            nc.vector.scalar_tensor_tensor(
+                hidden[o, edges[0]][:], acc[:], 0.0, gates[:, edges[0] : edges[-1]], MAX, MULT
             )
 
+        def cells(window, lo, hi):
+            return window[:].indirect(cell_list[:, lo // 16 : hi // 16])
+
         gather_words(0, 128)
-        gather_words(128, S)
         for o in (2, 3):
             first_layer(o, 0, 128)
+            nc.scalar.activation(cells(narrow[o], 0, 128), hidden[o, 0][:], COPY)
+        gather_words(128, S)
         quantize_w1(0, "second")
         for o in (2, 3):
             first_layer(o, 128, 384, S)
-        for o in (0, 1):
-            first_layer(o, 0, S)
-        wide[1] = keep.tile([P, 2 * V], F32, name="wide1", align_bytes=64, tag="last")
-        nc.scalar.copy(wide[1][:, :V], zero[:, 0:1].to_broadcast([P, V]))
-        scatter(narrow[2], 2, 0, 128)
-        scatter(narrow[3], 3, 0, 128)
-        scatter(narrow[2], 2, 128, S)
-        scatter(narrow[3], 3, 128, S)
-        nc.scalar.copy(wide[0][:, V:], narrow[2][:])
-        nc.scalar.copy(wide[1][:, V:], narrow[3][:])
-        scatter(wide[0], 0, 0, S)
+            nc.scalar.activation(cells(narrow[o], 128, S), hidden[o, 128][:], COPY)
+        for a in (0, 1):
+            first_layer(a, 0, S)
+        for a in (0, 1):
+            nc.vector.tensor_copy(cells(wide[a], 0, 256), hidden[a, 0][:, :256])
+        for a in (0, 1):
+            nc.vector.tensor_copy(wide[a][:, V:], narrow[a + 2][:])
+            nc.scalar.activation(cells(wide[a], 256, S), hidden[a, 0][:, 256:], COPY)
 
         w2_grouped = keep.tile([P, N, PACK], BF16, align_bytes=64)
-        nc.scalar.copy(
+        nc.vector.tensor_copy(
             w2_grouped[:].rearrange("p n (a e) -> p n a e", e=2), w2_raw[:].rearrange("p (e a) n -> p n a e", e=2)
         )
 
@@ -142,12 +144,10 @@ def tile_picked_voxel_relu_p_kernel(tc, x_words, x_scales, w1, w2, gate, offs, p
         def interleave(copy, a, lo, hi):
             copy(z_grouped[:, lo:hi, 2 * a : 2 * a + 2], wide[a][:].rearrange("p (e v) -> p v e", e=2)[:, lo:hi, :])
 
-        interleave(nc.scalar.copy, 0, 0, V // 2)
-        interleave(nc.scalar.copy, 0, V // 2, V)
-        scatter(wide[1], 1, 0, S)
-        w2_codes = keep.tile([P, N], U32, align_bytes=64, tag="hidden0")
+        w2_codes = keep.tile([P, N], U32, align_bytes=64)
         w2_plane = keep.tile([P, N], U8, align_bytes=64)
         quantize(w2_codes, w2_plane, w2_grouped, 0, N)
+        interleave(nc.vector.tensor_copy, 0, 0, V)
         z_codes = keep.tile([P, V], U32, align_bytes=64)
         z_plane = keep.tile([P, V], U8, align_bytes=64)
         result = keep.tile([P, V], F32)

@@ -15,6 +15,7 @@ FP8X4 = mybir.dt.float8_e4m3fn_x4
 COPY = mybir.ActivationFunctionType.Copy
 MAX = mybir.AluOpType.max
 MULT = mybir.AluOpType.mult
+ADD = mybir.AluOpType.add
 
 P = 128
 PACK = 4
@@ -57,19 +58,19 @@ def tile_picked_voxel_relu_p_kernel(tc, x_words, x_scales, w1, w2, gate, offs, p
             queue.dma_start(scale_rows[32 * q : 32 * q + 4, :], x_scales[0, 4 * q : 4 * q + 4, :].bitcast(I32))
         nc.sync.dma_start(w1_raw[:], w1.rearrange("(p j) c -> p j c", j=PACK))
         nc.sync.dma_start(word_table[:], x_words[0].rearrange("p c r -> p (c r)").bitcast(I32))
-        nc.sync.dma_start(cell_list[:], pos1)
         nc.sync.dma_start(gates[:, :256], gate[:, :256])
+        nc.sync.dma_start(cell_list[:], pos1)
         nc.sync.dma_start(gates[:, 256:], gate[:, 256:])
 
-        narrow = {o: keep.tile([P, V], F32, name="narrow%d" % o) for o in (2, 3)}
-        wide = {a: keep.tile([P, 2 * V], F32, name="wide%d" % a) for a in (0, 1)}
+        narrow = {o: keep.tile([P, V], F32, name="narrow%d" % o, align_bytes=64) for o in (1, 3)}
+        wide = {o: keep.tile([P, 2 * V], F32, name="wide%d" % o) for o in (0, 2)}
         zero = keep.tile([P, 8], F32)
         nc.vector.memset(zero[:], 0.0)
         nc.vector.memset(scale_table[:], 0)
-        nc.vector.memset(narrow[2][:], 0.0)
+        nc.vector.memset(narrow[1][:], 0.0)
         nc.vector.memset(wide[0][:, :V], 0.0)
         nc.scalar.activation(narrow[3][:], zero[:, 0:1].to_broadcast([P, V]), COPY)
-        nc.scalar.activation(wide[1][:, :V], zero[:, 0:1].to_broadcast([P, V]), COPY)
+        nc.scalar.activation(wide[2][:, :V], zero[:, 0:1].to_broadcast([P, V]), COPY)
 
         for q in range(4):
             nc.vector.tensor_copy(scale_table[32 * q : 32 * q + 4, :], scale_rows[32 * q : 32 * q + 4, :])
@@ -105,8 +106,8 @@ def tile_picked_voxel_relu_p_kernel(tc, x_words, x_scales, w1, w2, gate, offs, p
 
         hidden = {}
 
-        def first_layer(o, *edges, tag=""):
-            hidden[o, edges[0]] = keep.tile([P, edges[-1] - edges[0]], F32, name="hidden%d_%d" % (o, edges[0]), tag=tag)
+        def first_layer(o, *edges):
+            hidden[o, edges[0]] = keep.tile([P, edges[-1] - edges[0]], F32, name="hidden%d_%d" % (o, edges[0]), align_bytes=64)
             acc = psum.tile([P, edges[-1] - edges[0]], F32, name="acc")
             for lo, hi in zip(edges, edges[1:]):
                 product(acc[:, lo - edges[0] : hi - edges[0]], w1_codes[o - o % 2], w1_plane[o - o % 2], slice(P * (o % 2), P * (o % 2 + 1)), x_codes, x_plane, lo, hi)
@@ -118,36 +119,39 @@ def tile_picked_voxel_relu_p_kernel(tc, x_words, x_scales, w1, w2, gate, offs, p
             return window[:].indirect(cell_list[:, lo // 16 : hi // 16])
 
         gather_words(0, 128)
-        for o in (2, 3):
-            first_layer(o, 0, 128)
-            nc.scalar.activation(cells(narrow[o], 0, 128), hidden[o, 0][:], COPY)
-        gather_words(128, S)
+        gather_words(128, 256)
+        first_layer(3, 0, 128)
+        nc.scalar.activation(cells(narrow[3], 0, 128), hidden[3, 0][:], COPY)
+        first_layer(2, 0, 256)
+        nc.scalar.activation(cells(wide[2], 0, 256), hidden[2, 0][:], COPY)
+        gather_words(256, S)
         quantize_w1(0, "second")
-        for o in (2, 3):
-            first_layer(o, 128, 384, S)
-            nc.scalar.activation(cells(narrow[o], 128, S), hidden[o, 128][:], COPY)
-        for a in (0, 1):
-            first_layer(a, 0, S)
-        for a in (0, 1):
-            nc.vector.tensor_copy(cells(wide[a], 0, 256), hidden[a, 0][:, :256])
-        for a in (0, 1):
-            nc.vector.tensor_copy(wide[a][:, V:], narrow[a + 2][:])
-            nc.scalar.activation(cells(wide[a], 256, S), hidden[a, 0][:, 256:], COPY)
+        first_layer(3, 128, 256, S)
+        first_layer(2, 256, S)
+        nc.vector.tensor_copy(cells(narrow[3], 128, 256), hidden[3, 128][:, :128])
+        nc.scalar.activation(cells(narrow[3], 256, S), hidden[3, 128][:, 128:], COPY)
 
-        w2_grouped = keep.tile([P, N, PACK], BF16, align_bytes=64)
-        nc.vector.tensor_copy(
-            w2_grouped[:].rearrange("p n (a e) -> p n a e", e=2), w2_raw[:].rearrange("p (e a) n -> p n a e", e=2)
-        )
+        nc.gpsimd.tensor_scalar(wide[2][:, V:], narrow[3][:], 1.0, 0.0, MULT, ADD)
+        w2_grouped = keep.tile([P, N, PACK], BF16, align_bytes=64, tag="narrow3")
+        nc.gpsimd.tensor_scalar(w2_grouped[:], w2_raw[:].rearrange("p j n -> p n j"), 1.0, 0.0, MULT, ADD)
 
-        z_grouped = keep.tile([P, V, PACK], BF16, align_bytes=64)
-
-        def interleave(copy, a, lo, hi):
-            copy(z_grouped[:, lo:hi, 2 * a : 2 * a + 2], wide[a][:].rearrange("p (e v) -> p v e", e=2)[:, lo:hi, :])
-
+        first_layer(1, 0, S)
+        first_layer(0, 0, S)
+        nc.scalar.activation(cells(wide[0], 0, 256), hidden[0, 0][:, :256], COPY)
+        nc.vector.tensor_copy(cells(narrow[1], 0, S), hidden[1, 0][:])
         w2_codes = keep.tile([P, N], U32, align_bytes=64)
         w2_plane = keep.tile([P, N], U8, align_bytes=64)
         quantize(w2_codes, w2_plane, w2_grouped, 0, N)
-        interleave(nc.vector.tensor_copy, 0, 0, V)
+        nc.scalar.activation(cells(wide[2], 256, S), hidden[2, 256][:], COPY)
+        nc.vector.tensor_copy(wide[0][:, V:], narrow[1][:])
+        nc.scalar.activation(cells(wide[0], 256, S), hidden[0, 0][:, 256:], COPY)
+
+        z_grouped = keep.tile([P, V, PACK], BF16, align_bytes=64, tag="narrow1")
+
+        def interleave(copy, o, lo, hi):
+            copy(z_grouped[:, lo:hi, o : o + 2], wide[o][:].rearrange("p (e v) -> p v e", e=2)[:, lo:hi, :])
+
+        interleave(nc.vector.tensor_copy, 2, 0, V)
         z_codes = keep.tile([P, V], U32, align_bytes=64)
         z_plane = keep.tile([P, V], U8, align_bytes=64)
         result = keep.tile([P, V], F32)
@@ -164,12 +168,12 @@ def tile_picked_voxel_relu_p_kernel(tc, x_words, x_scales, w1, w2, gate, offs, p
         def store(lo, hi):
             nc.sync.dma_start(out[:, lo:hi], result[:, lo:hi])
 
-        interleave(nc.vector.tensor_copy, 1, 0, 256)
-        interleave(nc.scalar.copy, 1, 480, 512)
-        interleave(nc.vector.tensor_copy, 1, 256, 480)
-        interleave(nc.scalar.copy, 1, 512, 768)
-        interleave(nc.scalar.copy, 1, 768, 896)
-        interleave(nc.scalar.copy, 1, 896, 1024)
+        interleave(nc.vector.tensor_copy, 0, 0, 256)
+        interleave(nc.scalar.copy, 0, 480, 512)
+        interleave(nc.vector.tensor_copy, 0, 256, 480)
+        interleave(nc.scalar.copy, 0, 512, 768)
+        interleave(nc.scalar.copy, 0, 768, 896)
+        interleave(nc.scalar.copy, 0, 896, 1024)
         quantize_z(0, 256)
         second_layer(nc.scalar.copy, 0, 256)
         store(0, 256)

@@ -52,6 +52,7 @@ def tile_picked_voxel_relu_p_kernel(tc, x_words, x_scales, w1, w2, gate, offs, p
         scale_table = keep.tile([P, T // 4], I32, align_bytes=64)
         w1_raw = keep.tile([P, PACK, H], F32)
         gates = keep.tile([P, S], F32)
+        w2_raw = keep.tile([P, PACK, N], F32)
 
         nc.sync.dma_start(point_list[:], offs)
         for q, queue in enumerate((nc.sync, nc.scalar, nc.sync, nc.scalar)):
@@ -59,6 +60,7 @@ def tile_picked_voxel_relu_p_kernel(tc, x_words, x_scales, w1, w2, gate, offs, p
         nc.sync.dma_start(w1_raw[:], w1.rearrange("(p j) c -> p j c", j=PACK))
         nc.sync.dma_start(word_table[:], x_words[0].rearrange("p c r -> p (c r)").bitcast(I32))
         nc.sync.dma_start(gates[:, :256], gate[:, :256])
+        nc.sync.dma_start(w2_raw[:], w2.rearrange("(p j) n -> p j n", j=PACK))
         nc.sync.dma_start(cell_list[:], pos1)
         nc.sync.dma_start(gates[:, 256:], gate[:, 256:])
 
@@ -98,8 +100,8 @@ def tile_picked_voxel_relu_p_kernel(tc, x_words, x_scales, w1, w2, gate, offs, p
         group_w1(nc.scalar.copy, 0, 0, P)
         quantize_w1(2, "early")
 
-        w2_raw = keep.tile([P, PACK, N], F32)
-        nc.sync.dma_start(w2_raw[:], w2.rearrange("(p j) n -> p j n", j=PACK))
+        w2_grouped = keep.tile([P, N, PACK], BF16, align_bytes=64)
+        nc.scalar.copy(w2_grouped[:], w2_raw[:].rearrange("p j n -> p n j"))
 
         def gather_words(lo, hi):
             nc.vector.tensor_copy(x_codes[:, lo:hi], word_table[:].bitcast(U32).indirect(point_list[:, lo // 16 : hi // 16]))
@@ -132,8 +134,6 @@ def tile_picked_voxel_relu_p_kernel(tc, x_words, x_scales, w1, w2, gate, offs, p
         nc.scalar.activation(cells(narrow[3], 256, S), hidden[3, 128][:, 128:], COPY)
 
         nc.gpsimd.tensor_scalar(wide[2][:, V:], narrow[3][:], 1.0, 0.0, MULT, ADD)
-        w2_grouped = keep.tile([P, N, PACK], BF16, align_bytes=64, tag="narrow3")
-        nc.gpsimd.tensor_scalar(w2_grouped[:], w2_raw[:].rearrange("p j n -> p n j"), 1.0, 0.0, MULT, ADD)
 
         first_layer(1, 0, S)
         first_layer(0, 0, S)

@@ -108,8 +108,8 @@ def tile_picked_voxel_relu_p_kernel(tc, x_words, x_scales, w1, w2, gate, offs, p
 
         hidden = {}
 
-        def first_layer(o, *edges):
-            hidden[o, edges[0]] = keep.tile([P, edges[-1] - edges[0]], F32, name="hidden%d_%d" % (o, edges[0]), align_bytes=64)
+        def first_layer(o, *edges, tag=""):
+            hidden[o, edges[0]] = keep.tile([P, edges[-1] - edges[0]], F32, name="hidden%d_%d" % (o, edges[0]), align_bytes=64, tag=tag)
             acc = psum.tile([P, edges[-1] - edges[0]], F32, name="acc")
             for lo, hi in zip(edges, edges[1:]):
                 product(acc[:, lo - edges[0] : hi - edges[0]], w1_codes[o - o % 2], w1_plane[o - o % 2], slice(P * (o % 2), P * (o % 2 + 1)), x_codes, x_plane, lo, hi)
@@ -136,17 +136,18 @@ def tile_picked_voxel_relu_p_kernel(tc, x_words, x_scales, w1, w2, gate, offs, p
         nc.gpsimd.tensor_scalar(wide[2][:, V:], narrow[3][:], 1.0, 0.0, MULT, ADD)
 
         first_layer(1, 0, S)
-        first_layer(0, 0, S)
-        nc.scalar.activation(cells(wide[0], 0, 256), hidden[0, 0][:, :256], COPY)
+        first_layer(0, 256, S)
+        nc.scalar.activation(cells(wide[0], 256, S), hidden[0, 256][:], COPY)
         nc.vector.tensor_copy(cells(narrow[1], 0, S), hidden[1, 0][:])
+        first_layer(0, 0, 256, tag="hidden3_128")
         w2_codes = keep.tile([P, N], U32, align_bytes=64)
         w2_plane = keep.tile([P, N], U8, align_bytes=64)
         quantize(w2_codes, w2_plane, w2_grouped, 0, N)
         nc.scalar.activation(cells(wide[2], 256, S), hidden[2, 256][:], COPY)
         nc.vector.tensor_copy(wide[0][:, V:], narrow[1][:])
-        nc.scalar.activation(cells(wide[0], 256, S), hidden[0, 0][:, 256:], COPY)
+        nc.scalar.activation(cells(wide[0], 0, 256), hidden[0, 0][:], COPY)
 
-        z_grouped = keep.tile([P, V, PACK], BF16, align_bytes=64, tag="narrow1")
+        z_grouped = keep.tile([P, V, PACK], BF16, align_bytes=64)
 
         def interleave(copy, o, lo, hi):
             copy(z_grouped[:, lo:hi, o : o + 2], wide[o][:].rearrange("p (e v) -> p v e", e=2)[:, lo:hi, :])

@@ -61,8 +61,8 @@ def tile_picked_voxel_relu_p_kernel(tc, x_words, x_scales, w1, w2, gate, offs, p
         nc.sync.dma_start(word_table[:], x_words[0].rearrange("p c r -> p (c r)").bitcast(I32))
         nc.sync.dma_start(gates[:, :256], gate[:, :256])
         nc.sync.dma_start(w2_raw[:], w2.rearrange("(p j) n -> p j n", j=PACK))
-        nc.sync.dma_start(cell_list[:], pos1)
         nc.sync.dma_start(gates[:, 256:], gate[:, 256:])
+        nc.sync.dma_start(cell_list[:], pos1)
 
         narrow = {o: keep.tile([P, V], F32, name="narrow%d" % o, align_bytes=64) for o in (1, 3)}
         wide = {o: keep.tile([P, 2 * V], F32, name="wide%d" % o) for o in (0, 2)}
@@ -100,9 +100,6 @@ def tile_picked_voxel_relu_p_kernel(tc, x_words, x_scales, w1, w2, gate, offs, p
         group_w1(nc.scalar.copy, 0, 0, P)
         quantize_w1(2, "early")
 
-        w2_grouped = keep.tile([P, N, PACK], BF16, align_bytes=64)
-        nc.scalar.copy(w2_grouped[:], w2_raw[:].rearrange("p j n -> p n j"))
-
         def gather_words(lo, hi):
             nc.vector.tensor_copy(x_codes[:, lo:hi], word_table[:].bitcast(U32).indirect(point_list[:, lo // 16 : hi // 16]))
 
@@ -127,9 +124,11 @@ def tile_picked_voxel_relu_p_kernel(tc, x_words, x_scales, w1, w2, gate, offs, p
         first_layer(2, 0, 256)
         nc.scalar.activation(cells(wide[2], 0, 256), hidden[2, 0][:], COPY)
         gather_words(256, S)
-        quantize_w1(0, "second")
+        w2_grouped = keep.tile([P, N, PACK], BF16, align_bytes=64, tag="word_table")
+        nc.gpsimd.tensor_scalar(w2_grouped[:], w2_raw[:].rearrange("p j n -> p n j"), 1.0, 0.0, MULT, ADD)
         first_layer(3, 128, 256, S)
         first_layer(2, 256, S)
+        quantize_w1(0, "hidden3_0")
         nc.vector.tensor_copy(cells(narrow[3], 128, 256), hidden[3, 128][:, :128])
         nc.scalar.activation(cells(narrow[3], 256, S), hidden[3, 128][:, 128:], COPY)
 
@@ -140,7 +139,7 @@ def tile_picked_voxel_relu_p_kernel(tc, x_words, x_scales, w1, w2, gate, offs, p
         nc.scalar.activation(cells(wide[0], 256, S), hidden[0, 256][:], COPY)
         nc.vector.tensor_copy(cells(narrow[1], 0, S), hidden[1, 0][:])
         first_layer(0, 0, 256, tag="hidden3_128")
-        w2_codes = keep.tile([P, N], U32, align_bytes=64)
+        w2_codes = keep.tile([P, N], U32, align_bytes=64, tag="hidden0_256")
         w2_plane = keep.tile([P, N], U8, align_bytes=64)
         quantize(w2_codes, w2_plane, w2_grouped, 0, N)
         nc.scalar.activation(cells(wide[2], 256, S), hidden[2, 256][:], COPY)

@@ -60,13 +60,13 @@ def tile_picked_voxel_relu_p_kernel(tc, x_words, x_scales, w1, w2, gate, offs, p
         nc.sync.dma_start(w1_raw[:], w1.rearrange("(p j) c -> p j c", j=PACK))
         nc.sync.dma_start(word_table[:], x_words[0].rearrange("p c r -> p (c r)").bitcast(I32))
         nc.sync.dma_start(gates[:, :256], gate[:, :256])
+        nc.sync.dma_start(cell_list[:], pos1)
         nc.sync.dma_start(w2_raw[:], w2.rearrange("(p j) n -> p j n", j=PACK))
         nc.sync.dma_start(gates[:, 256:], gate[:, 256:])
-        nc.sync.dma_start(cell_list[:], pos1)
 
         narrow = {o: keep.tile([P, V], F32, name="narrow%d" % o, align_bytes=64) for o in (1, 3)}
         wide = {o: keep.tile([P, 2 * V], F32, name="wide%d" % o) for o in (0, 2)}
-        zero = keep.tile([P, 8], F32)
+        zero = keep.tile([P, 8], F32, align_bytes=64)
         nc.vector.memset(zero[:], 0.0)
         nc.vector.memset(scale_table[:], 0)
         nc.vector.memset(narrow[1][:], 0.0)
@@ -105,13 +105,13 @@ def tile_picked_voxel_relu_p_kernel(tc, x_words, x_scales, w1, w2, gate, offs, p
 
         hidden = {}
 
-        def first_layer(o, *edges, tag=""):
+        def first_layer(o, *edges, tag="", floor=0.0):
             hidden[o, edges[0]] = keep.tile([P, edges[-1] - edges[0]], F32, name="hidden%d_%d" % (o, edges[0]), align_bytes=64, tag=tag)
             acc = psum.tile([P, edges[-1] - edges[0]], F32, name="acc")
             for lo, hi in zip(edges, edges[1:]):
                 product(acc[:, lo - edges[0] : hi - edges[0]], w1_codes[o - o % 2], w1_plane[o - o % 2], slice(P * (o % 2), P * (o % 2 + 1)), x_codes, x_plane, lo, hi)
             nc.vector.scalar_tensor_tensor(
-                hidden[o, edges[0]][:], acc[:], 0.0, gates[:, edges[0] : edges[-1]], MAX, MULT
+                hidden[o, edges[0]][:], acc[:], floor, gates[:, edges[0] : edges[-1]], MAX, MULT
             )
 
         def cells(window, lo, hi):
@@ -119,16 +119,16 @@ def tile_picked_voxel_relu_p_kernel(tc, x_words, x_scales, w1, w2, gate, offs, p
 
         gather_words(0, 128)
         gather_words(128, 256)
-        first_layer(3, 0, 128)
+        first_layer(3, 0, 128, floor=zero[:, 0:1])
         nc.scalar.activation(cells(narrow[3], 0, 128), hidden[3, 0][:], COPY)
         first_layer(2, 0, 256)
         nc.scalar.activation(cells(wide[2], 0, 256), hidden[2, 0][:], COPY)
         gather_words(256, S)
-        w2_grouped = keep.tile([P, N, PACK], BF16, align_bytes=64, tag="word_table")
+        quantize_w1(0, "zero")
+        w2_grouped = keep.tile([P, N, PACK], BF16, align_bytes=64, tag="w1_grouped")
         nc.gpsimd.tensor_scalar(w2_grouped[:], w2_raw[:].rearrange("p j n -> p n j"), 1.0, 0.0, MULT, ADD)
         first_layer(3, 128, 256, S)
         first_layer(2, 256, S)
-        quantize_w1(0, "hidden3_0")
         nc.vector.tensor_copy(cells(narrow[3], 128, 256), hidden[3, 128][:, :128])
         nc.scalar.activation(cells(narrow[3], 256, S), hidden[3, 128][:, 128:], COPY)
 
@@ -139,52 +139,49 @@ def tile_picked_voxel_relu_p_kernel(tc, x_words, x_scales, w1, w2, gate, offs, p
         nc.scalar.activation(cells(wide[0], 256, S), hidden[0, 256][:], COPY)
         nc.vector.tensor_copy(cells(narrow[1], 0, S), hidden[1, 0][:])
         first_layer(0, 0, 256, tag="hidden3_128")
-        w2_codes = keep.tile([P, N], U32, align_bytes=64, tag="hidden0_256")
-        w2_plane = keep.tile([P, N], U8, align_bytes=64)
-        quantize(w2_codes, w2_plane, w2_grouped, 0, N)
         nc.scalar.activation(cells(wide[2], 256, S), hidden[2, 256][:], COPY)
         nc.vector.tensor_copy(wide[0][:, V:], narrow[1][:])
         nc.scalar.activation(cells(wide[0], 0, 256), hidden[0, 0][:], COPY)
 
-        z_grouped = keep.tile([P, V, PACK], BF16, align_bytes=64)
+        z_first = keep.tile([P, 256, PACK], BF16, align_bytes=64)
+        z_rest = keep.tile([P, V - 256, PACK], BF16, align_bytes=64)
+
+        def z_grouped(lo, hi):
+            return z_first[:, lo:hi, :] if hi <= 256 else z_rest[:, lo - 256 : hi - 256, :]
 
         def interleave(copy, o, lo, hi):
-            copy(z_grouped[:, lo:hi, o : o + 2], wide[o][:].rearrange("p (e v) -> p v e", e=2)[:, lo:hi, :])
+            copy(z_grouped(lo, hi)[:, :, o : o + 2], wide[o][:].rearrange("p (e v) -> p v e", e=2)[:, lo:hi, :])
 
-        interleave(nc.vector.tensor_copy, 2, 0, V)
-        z_codes = keep.tile([P, V], U32, align_bytes=64)
+        interleave(nc.vector.tensor_copy, 2, 0, 256)
+        interleave(nc.vector.tensor_copy, 2, 256, V)
+        w2_codes = keep.tile([P, N], U32, align_bytes=64, tag="narrow1")
+        w2_plane = keep.tile([P, N], U8, align_bytes=64)
+        quantize(w2_codes, w2_plane, w2_grouped, 0, N)
         z_plane = keep.tile([P, V], U8, align_bytes=64)
         result = keep.tile([P, V], F32)
 
-        def quantize_z(lo, hi):
-            quantize(z_codes, z_plane, z_grouped, lo, hi)
-
-        def second_layer(copy, *edges):
-            acc = psum.tile([P, edges[-1] - edges[0]], F32, name="acc")
-            for lo, hi in zip(edges, edges[1:]):
-                product(acc[:, lo - edges[0] : hi - edges[0]], w2_codes, w2_plane, slice(0, N), z_codes, z_plane, lo, hi)
-            copy(result[:, edges[0] : edges[-1]], acc[:])
+        def second_layer(copy, z_codes, lo, hi):
+            quantize(z_codes, z_plane[:, lo:hi], z_grouped(lo, hi), 0, hi - lo)
+            acc = psum.tile([P, hi - lo], F32, name="acc")
+            product(acc[:], w2_codes, w2_plane, slice(0, N), z_codes, z_plane[:, lo:hi], 0, hi - lo)
+            copy(result[:, lo:hi], acc[:])
 
         def store(lo, hi):
             nc.sync.dma_start(out[:, lo:hi], result[:, lo:hi])
 
         interleave(nc.vector.tensor_copy, 0, 0, 256)
-        interleave(nc.scalar.copy, 0, 480, 512)
-        interleave(nc.vector.tensor_copy, 0, 256, 480)
+        interleave(nc.vector.tensor_copy, 0, 256, 512)
         interleave(nc.scalar.copy, 0, 512, 768)
         interleave(nc.scalar.copy, 0, 768, 896)
         interleave(nc.scalar.copy, 0, 896, 1024)
-        quantize_z(0, 256)
-        second_layer(nc.scalar.copy, 0, 256)
+        low_codes = keep.tile([P, V // 2], U32, align_bytes=64)
+        second_layer(nc.scalar.copy, low_codes[:, :256], 0, 256)
         store(0, 256)
-        quantize_z(256, 512)
-        second_layer(nc.scalar.copy, 256, 512)
+        second_layer(nc.scalar.copy, low_codes[:, 256:], 256, 512)
         store(256, 512)
-        quantize_z(512, 768)
-        second_layer(nc.scalar.copy, 512, 768)
+        high_codes = keep.tile([P, V // 2], U32, align_bytes=64, tag="z_first")
+        second_layer(nc.scalar.copy, high_codes[:, :256], 512, 768)
         store(512, 768)
-        quantize_z(768, 896)
-        second_layer(nc.vector.tensor_copy, 768, 896)
-        quantize_z(896, 1024)
-        second_layer(nc.vector.tensor_copy, 896, 1024)
+        second_layer(nc.vector.tensor_copy, high_codes[:, 256:384], 768, 896)
+        second_layer(nc.vector.tensor_copy, high_codes[:, 384:], 896, 1024)
         store(768, 1024)

from contextlib import ExitStack

import concourse.mybir as mybir

K, T, S, V, H, N = 512, 1024, 512, 1024, 512, 128
FLOPS = 2 * K * H * S + 2 * H * N * V

F32 = mybir.dt.float32
BF16 = mybir.dt.bfloat16
I32 = mybir.dt.int32
U32 = mybir.dt.uint32
U16 = mybir.dt.uint16
U8 = mybir.dt.uint8
FP8X4 = mybir.dt.float8_e4m3fn_x4
COPY = mybir.ActivationFunctionType.Copy
MAX = mybir.AluOpType.max
MULT = mybir.AluOpType.mult
ADD = mybir.AluOpType.add

P = 128
PACK = 4


def tile_picked_voxel_relu_p_kernel(tc, x_words, x_scales, w1, w2, gate, offs, pos1, out):
    nc = tc.nc
    with ExitStack() as ctx:
        keep = ctx.enter_context(tc.tile_pool(name="keep", bufs=1))
        psum = ctx.enter_context(tc.psum_pool(name="psum", bufs=8))

        def quantize(codes, plane, grouped, lo, hi):
            nc.vector.quantize_mx(
                out=codes[:, lo:hi].bitcast(FP8X4),
                scales=plane[:, lo:hi],
                in_=grouped[:, lo:hi, :].rearrange("p c j -> p (c j)"),
            )

        def product(acc, w_codes, w_plane, w_cols, codes, plane, lo, hi):
            nc.tensor.matmul_mx(
                out=acc,
                lhsT=w_codes[:, w_cols].bitcast(FP8X4),
                lhsT_scale=w_plane[:, w_cols],
                rhs=codes[:, lo:hi].bitcast(FP8X4),
                rhs_scale=plane[:, lo:hi],
                start=True,
                stop=True,
            )

        point_list = keep.tile([P, S // 16], U16)
        cell_list = keep.tile([P, S // 16], U16)
        word_table = keep.tile([P, T], I32, align_bytes=64)
        scale_rows = keep.tile([P, T // 4], I32, align_bytes=64)
        scale_table = keep.tile([P, T // 4], I32, align_bytes=64)
        w1_raw = keep.tile([P, PACK, H], F32)
        gates = keep.tile([P, S], F32)
        w2_raw = keep.tile([P, PACK, N], F32)

        nc.sync.dma_start(point_list[:], offs)
        for q, queue in enumerate((nc.sync, nc.scalar, nc.sync, nc.scalar)):
            queue.dma_start(scale_rows[32 * q : 32 * q + 4, :], x_scales[0, 4 * q : 4 * q + 4, :].bitcast(I32))
        nc.sync.dma_start(w1_raw[:], w1.rearrange("(p j) c -> p j c", j=PACK))
        nc.sync.dma_start(word_table[:], x_words[0].rearrange("p c r -> p (c r)").bitcast(I32))
        nc.sync.dma_start(gates[:, :256], gate[:, :256])
        nc.sync.dma_start(cell_list[:], pos1)
        nc.sync.dma_start(w2_raw[:], w2.rearrange("(p j) n -> p j n", j=PACK))
        nc.sync.dma_start(gates[:, 256:], gate[:, 256:])

        narrow = {o: keep.tile([P, V], F32, name="narrow%d" % o, align_bytes=64) for o in (1, 3)}
        wide = {o: keep.tile([P, 2 * V], F32, name="wide%d" % o) for o in (0, 2)}
        zero = keep.tile([P, 8], F32, align_bytes=64)
        nc.vector.memset(zero[:], 0.0)
        nc.vector.memset(scale_table[:], 0)
        nc.vector.memset(narrow[1][:], 0.0)
        nc.vector.memset(wide[0][:, :V], 0.0)
        nc.scalar.activation(narrow[3][:], zero[:, 0:1].to_broadcast([P, V]), COPY)
        nc.scalar.activation(wide[2][:, :V], zero[:, 0:1].to_broadcast([P, V]), COPY)

        for q in range(4):
            nc.vector.tensor_copy(scale_table[32 * q : 32 * q + 4, :], scale_rows[32 * q : 32 * q + 4, :])
        x_codes = keep.tile([P, S], U32, align_bytes=64)
        x_plane = keep.tile([P, S], U8, align_bytes=64)
        nc.vector.tensor_copy(x_plane[:], scale_table[:].bitcast(U8).indirect(point_list[:]))

        w1_grouped = keep.tile([P, H, PACK], BF16, align_bytes=64)

        def group_w1(copy, o, lo, hi):
            copy(
                w1_grouped[:].rearrange("p (o m) j -> p m j o", o=PACK)[:, lo:hi, :, o : o + 2],
                w1_raw[:].rearrange("p j (m o) -> p m j o", o=PACK)[:, lo:hi, :, o : o + 2],
            )

        w1_codes, w1_plane = {}, {}

        def quantize_w1(o, tag):
            w1_codes[o] = keep.tile([P, 2 * P], U32, align_bytes=64, name="w1_codes%d" % o, tag=tag)
            w1_plane[o] = keep.tile([P, 2 * P], U8, align_bytes=64, name="w1_plane%d" % o)
            quantize(w1_codes[o], w1_plane[o], w1_grouped[:, P * o : P * (o + 2), :], 0, 2 * P)

        group_w1(nc.vector.tensor_copy, 2, 0, 84)
        group_w1(nc.scalar.copy, 2, 84, P)
        group_w1(nc.scalar.copy, 0, 0, P)
        quantize_w1(2, "early")

        def gather_words(lo, hi):
            nc.vector.tensor_copy(x_codes[:, lo:hi], word_table[:].bitcast(U32).indirect(point_list[:, lo // 16 : hi // 16]))

        hidden = {}

        def first_layer(o, *edges, tag="", floor=0.0):
            hidden[o, edges[0]] = keep.tile([P, edges[-1] - edges[0]], F32, name="hidden%d_%d" % (o, edges[0]), align_bytes=64, tag=tag)
            acc = psum.tile([P, edges[-1] - edges[0]], F32, name="acc")
            for lo, hi in zip(edges, edges[1:]):
                product(acc[:, lo - edges[0] : hi - edges[0]], w1_codes[o - o % 2], w1_plane[o - o % 2], slice(P * (o % 2), P * (o % 2 + 1)), x_codes, x_plane, lo, hi)
            nc.vector.scalar_tensor_tensor(
                hidden[o, edges[0]][:], acc[:], floor, gates[:, edges[0] : edges[-1]], MAX, MULT
            )

        def cells(window, lo, hi):
            return window[:].indirect(cell_list[:, lo // 16 : hi // 16])

        gather_words(0, 128)
        gather_words(128, 256)
        first_layer(3, 0, 128, floor=zero[:, 0:1])
        nc.scalar.activation(cells(narrow[3], 0, 128), hidden[3, 0][:], COPY)
        first_layer(2, 0, 256)
        nc.scalar.activation(cells(wide[2], 0, 256), hidden[2, 0][:], COPY)
        gather_words(256, S)
        quantize_w1(0, "zero")
        w2_grouped = keep.tile([P, N, PACK], BF16, align_bytes=64, tag="w1_grouped")
        nc.gpsimd.tensor_scalar(w2_grouped[:], w2_raw[:].rearrange("p j n -> p n j"), 1.0, 0.0, MULT, ADD)
        first_layer(3, 128, 256, S)
        first_layer(2, 256, S)
        nc.vector.tensor_copy(cells(narrow[3], 128, 256), hidden[3, 128][:, :128])
        nc.scalar.activation(cells(narrow[3], 256, S), hidden[3, 128][:, 128:], COPY)

        nc.gpsimd.tensor_scalar(wide[2][:, V:], narrow[3][:], 1.0, 0.0, MULT, ADD)

        first_layer(1, 0, S)
        first_layer(0, 256, S)
        nc.scalar.activation(cells(wide[0], 256, S), hidden[0, 256][:], COPY)
        nc.vector.tensor_copy(cells(narrow[1], 0, S), hidden[1, 0][:])
        first_layer(0, 0, 256, tag="hidden3_128")
        nc.scalar.activation(cells(wide[2], 256, S), hidden[2, 256][:], COPY)
        nc.vector.tensor_copy(wide[0][:, V:], narrow[1][:])
        nc.scalar.activation(cells(wide[0], 0, 256), hidden[0, 0][:], COPY)

        z_first = keep.tile([P, 256, PACK], BF16, align_bytes=64)
        z_rest = keep.tile([P, V - 256, PACK], BF16, align_bytes=64)

        def z_grouped(lo, hi):
            return z_first[:, lo:hi, :] if hi <= 256 else z_rest[:, lo - 256 : hi - 256, :]

        def interleave(copy, o, lo, hi):
            copy(z_grouped(lo, hi)[:, :, o : o + 2], wide[o][:].rearrange("p (e v) -> p v e", e=2)[:, lo:hi, :])

        interleave(nc.vector.tensor_copy, 2, 0, 256)
        interleave(nc.vector.tensor_copy, 2, 256, V)
        w2_codes = keep.tile([P, N], U32, align_bytes=64, tag="narrow1")
        w2_plane = keep.tile([P, N], U8, align_bytes=64)
        quantize(w2_codes, w2_plane, w2_grouped, 0, N)
        z_plane = keep.tile([P, V], U8, align_bytes=64)
        result = keep.tile([P, V], F32)

        def second_layer(copy, z_codes, lo, hi):
            quantize(z_codes, z_plane[:, lo:hi], z_grouped(lo, hi), 0, hi - lo)
            acc = psum.tile([P, hi - lo], F32, name="acc")
            product(acc[:], w2_codes, w2_plane, slice(0, N), z_codes, z_plane[:, lo:hi], 0, hi - lo)
            copy(result[:, lo:hi], acc[:])

        def store(lo, hi):
            nc.sync.dma_start(out[:, lo:hi], result[:, lo:hi])

        interleave(nc.vector.tensor_copy, 0, 0, 256)
        interleave(nc.vector.tensor_copy, 0, 256, 512)
        interleave(nc.scalar.copy, 0, 512, 768)
        interleave(nc.scalar.copy, 0, 768, 896)
        interleave(nc.scalar.copy, 0, 896, 1024)
        low_codes = keep.tile([P, V // 2], U32, align_bytes=64)
        second_layer(nc.scalar.copy, low_codes[:, :256], 0, 256)
        store(0, 256)
        second_layer(nc.scalar.copy, low_codes[:, 256:], 256, 512)
        store(256, 512)
        high_codes = keep.tile([P, V // 2], U32, align_bytes=64, tag="z_first")
        second_layer(nc.scalar.copy, high_codes[:, :256], 512, 768)
        store(512, 768)
        second_layer(nc.vector.tensor_copy, high_codes[:, 256:384], 768, 896)
        second_layer(nc.vector.tensor_copy, high_codes[:, 384:], 896, 1024)
        store(768, 1024)
